import numpy as np
import ml_dtypes


def mxq(x, axis, fmt="e4m3"):
    dtype, down = {"e4m3": (ml_dtypes.float8_e4m3fn, 7), "e5m2": (ml_dtypes.float8_e5m2, 14)}[fmt]
    v = np.moveaxis(np.asarray(x, np.float32).astype(ml_dtypes.bfloat16).astype(np.float64), axis, -1)
    blocks = v.reshape(v.shape[:-1] + (-1, 32))
    amax = np.abs(blocks).max(-1, keepdims=True)
    byte = np.maximum(np.where(amax > 0, np.frexp(amax)[1] - 1 + 127, 0) - down, 1)
    scale = np.exp2(byte - 127.0)
    codes = (blocks / scale).astype(np.float32).astype(dtype).astype(np.float64)
    return np.moveaxis((codes * scale).reshape(v.shape), -1, axis)


WIDE = False


def mx_kscale(k):
    if not WIDE:
        return np.ones(k)
    levels = np.array([10, -10, 5, -5, 0])
    if k % 512:
        return np.exp2(np.random.permutation(np.resize(levels, k // 32))).repeat(32)
    a = np.empty((k // 512, 16))
    for p in range(k // 512):
        a[p, :8] = np.random.permutation(np.resize(levels, 8))
        for g in range(8):
            far = levels[np.abs(levels - a[p, g]) >= 10]
            a[p, g + 8] = far[np.random.randint(len(far))]
    return np.exp2(a.ravel()).repeat(32)


def f64(x):
    return np.asarray(x).astype(np.float64)


def striped8(idx):
    return np.concatenate([v.reshape(-1, 16).T for v in idx]).astype(np.uint16)


def unstriped8(offs):
    return np.stack([offs[16 * g:16 * g + 16].T.reshape(-1) for g in range(8)]).astype(np.int64)


E2M1 = np.array([0.0, 0.5, 1.0, 1.5, 2.0, 3.0, 4.0, 6.0, -0.0, -0.5, -1.0, -1.5, -2.0, -3.0, -4.0, -6.0])


def pack_weight(w, fmt):
    k, n = w.shape
    w = f64(np.asarray(w, np.float32).astype(ml_dtypes.bfloat16)).reshape(k // 32, 32, n)
    amax = np.abs(w).max(1)
    if fmt == "e4m3":
        byte = np.frexp(amax)[1] - 1 + 127 - 7
    else:
        mant, ex = np.frexp(amax / 6.0)
        byte = np.where(mant > 0.5, ex, ex - 1) + 127
    byte = np.clip(np.where(amax > 0, byte, 1), 1, 254)
    scaled = (w * np.exp2(127.0 - byte)[:, None, :]).reshape(k, n).astype(np.float32)
    by_word = np.ascontiguousarray(scaled.reshape(k // 512, 128, 4, n).transpose(0, 1, 3, 2))
    if fmt == "e4m3":
        words = by_word.astype(ml_dtypes.float8_e4m3fn).view(np.uint8)
    else:
        c = by_word.astype(ml_dtypes.float4_e2m1fn).view(np.uint8) & 0xF
        words = (c[..., 0::2] | (c[..., 1::2] << 4)).reshape(k // 512, 128, 2 * n)
    return np.ascontiguousarray(words), np.ascontiguousarray(byte.astype(np.uint8).reshape(k // 512, 16, n))


def unpack_weight(words, scales, fmt):
    g, _, n = scales.shape
    words = np.ascontiguousarray(words).reshape(g, 128, n, -1)
    if fmt == "e4m3":
        vals = words.view(ml_dtypes.float8_e4m3fn).astype(np.float64)
    else:
        nib = np.empty((g, 128, n, 4), np.uint8)
        nib[..., 0::2] = words & 0xF
        nib[..., 1::2] = words >> 4
        vals = E2M1[nib]
    vals = vals * np.repeat(np.exp2(scales.astype(np.float64) - 127.0), 8, axis=1)[..., None]
    return vals.transpose(0, 1, 3, 2).reshape(g * 512, n)


K, R, M, T, S = 1024, 512, 1024, 1024, 512


def setup_inputs():
    n = np.random.standard_normal
    s = mx_kscale(K)[:, None]
    u = mx_kscale(R)[:, None]
    p_w4 = pack_weight(n((K, M)) / np.sqrt(K) / s, "e2m1")
    return {
        "xT": (n((K, T)) * s).astype(np.float32),
        "w4_words": p_w4[0],
        "w4_scales": p_w4[1],
        "down": (n((K, R)) / np.sqrt(K) / s * u.T).astype(np.float32),
        "up": (0.5 * n((R, M)) / np.sqrt(R) / u).astype(np.float32),
        "wgt": np.repeat(np.random.uniform(0.5, 2.0, (8, S)), 16, axis=0).astype(np.float32),
        "offs": striped8(np.stack([np.random.permutation(T)[:S] for _ in range(8)])),
    }


def reference(xT, w4_words, w4_scales, down, up, wgt, offs):
    idx = unstriped8(offs)
    group = np.arange(K) % 512 // 64
    xg = f64(wgt)[np.arange(K) // 4 % 128] * f64(xT)[np.arange(K)[:, None], idx[group]]
    xT_ = mxq(xg, 0, "e4m3")
    w4_ = unpack_weight(w4_words, w4_scales, "e2m1")
    down_ = mxq(f64(down), 0, "e4m3")
    up_ = mxq(f64(up), 0, "e4m3")
    h_ = mxq(down_.T @ xT_, 0, "e4m3")
    y = xT_.T @ w4_ + h_.T @ up_
    return y

@@ -1,0 +1,271 @@
+from contextlib import ExitStack
+
+import concourse.mybir as mybir
+
+K, R, M, T, S = 1024, 512, 1024, 1024, 512
+FLOPS = 2 * (K * R * S + K * M * S + R * M * S)
+
+F32 = mybir.dt.float32
+BF16 = mybir.dt.bfloat16
+I32 = mybir.dt.int32
+U32 = mybir.dt.uint32
+U16 = mybir.dt.uint16
+U8 = mybir.dt.uint8
+E4M3 = mybir.dt.float8_e4m3fn_x4
+E2M1 = mybir.dt.float4_e2m1fn_x4
+MULT = mybir.AluOpType.mult
+
+P = 128
+PASSES = K // 512
+HALF = S // 2
+NT = 512
+
+
+def tile_list_hlora_tm_none_kernel(tc, xT, w4_words, w4_scales, down, up, wgt, offs, out):
+    nc = tc.nc
+    with ExitStack() as ctx:
+        held = ctx.enter_context(tc.tile_pool(name="held", bufs=1))
+        keep = ctx.enter_context(tc.tile_pool(name="keep", bufs=1))
+        psum = ctx.enter_context(tc.psum_pool(name="psum", bufs=1))
+
+        offsets = held.tile([P, S // 16], U16, name="offsets")
+        nc.sync.dma_start(offsets[:], offs)
+
+        w4s = keep.tile([P, PASSES * M], U8, name="w4s", align_bytes=64)
+        nc.vector.memset(w4s[:].bitcast(I32), 0)
+        scale_rows = w4_scales.bitcast(I32).rearrange("a (q r) n -> r q a n", r=4)
+
+        wgt_t = keep.tile([P, S], F32, name="wgt_t")
+        x_rows = xT.rearrange("(a p i) t -> a i p t", a=PASSES, i=4)
+        down_rows = down.rearrange("(a p i) r -> a p i r", a=PASSES, i=4)
+        up_rows = up.rearrange("(p i) n -> p i n", i=4)
+        w4_rows = w4_words.bitcast(I32).rearrange("a p n -> p a n")
+        planes = [[keep.tile([P, T], F32, name=f"x{a}{i}") for i in range(4)] for a in range(PASSES)]
+        down_raw = [keep.tile([P, 4, R], F32, name=f"down{a}") for a in range(PASSES)]
+        up_raw = [keep.tile([P, 4, NT], F32, name=f"up{nh}") for nh in range(2)]
+        w4w = keep.tile([P, PASSES * 2 * M], U8, name="w4w", align_bytes=64)
+        w4_view = w4w[:].bitcast(I32).rearrange("p (a n) -> p a n", a=PASSES)
+        for what in ["x00","g00","x01","x02","x03","s00","w00","w10","x10","x11","d00","d01","x12","x13","d10","d11","u00","u10"]:
+            kind, u, v = what[0], int(what[1]), int(what[2])
+            if kind == "x":
+                nc.sync.dma_start(planes[u][v][:], x_rows[u, v])
+            if kind == "d":
+                nc.sync.dma_start(down_raw[u][:, :, v * 256 : v * 256 + 256], down_rows[u][:, :, v * 256 : v * 256 + 256])
+            if kind == "D":
+                nc.sync.dma_start(down_raw[u][:], down_rows[u])
+            if kind == "u":
+                nc.sync.dma_start(up_raw[u][:], up_rows[:, :, u * NT : (u + 1) * NT])
+            if kind == "w":
+                nc.sync.dma_start(w4_view[:, :, u * 256 : u * 256 + 256], w4_rows[:, :, u * 256 : u * 256 + 256])
+            if kind == "W":
+                nc.sync.dma_start(w4_view, w4_rows)
+            if kind == "g":
+                nc.sync.dma_start(wgt_t[:], wgt)
+            if kind == "s":
+                for r in range(4):
+                    nc.sync.dma_start(w4s[r:P:32, :].bitcast(I32).rearrange("q (a n) -> q a n", a=PASSES), scale_rows[r])
+
+        def gather(a, i, half, g):
+            nc.vector.tensor_tensor(
+                g[half][:, i, :],
+                planes[a][i][:].indirect(offsets[:, half * 16 : half * 16 + 16]),
+                wgt_t[:, half * HALF : (half + 1) * HALF],
+                MULT,
+            )
+
+        def copy_on(engine, dst, src):
+            if engine == "S":
+                nc.scalar.copy(dst, src)
+            else:
+                nc.vector.tensor_copy(dst, src)
+
+        def interleave(engine, name, src, width):
+            grouped = keep.tile([P, width, 4], BF16, name=name, align_bytes=64)
+            copy_on(
+                engine,
+                grouped[:].rearrange("p (c i) t -> p c t i", i=4),
+                src.rearrange("p t (c i) -> p c t i", i=4),
+            )
+            return grouped
+
+        def quantise(codes, scales, grouped):
+            nc.vector.quantize_mx(out=codes.bitcast(E4M3), scales=scales, in_=grouped)
+
+        xg_c, xg_s = [], []
+        for a in range(PASSES):
+            c = keep.tile([P, S], U32, name=f"xgc{a}", align_bytes=64)
+            s = keep.tile([P, S], U8, name=f"xgs{a}", align_bytes=64)
+            xg_c.append(c)
+            xg_s.append(s)
+        dn_c, dn_s = [], []
+        for a in range(PASSES):
+            c = keep.tile([P, R], U32, name=f"dnc{a}", align_bytes=64)
+            s = keep.tile([P, R], U8, name=f"dns{a}", align_bytes=64)
+            dn_c.append(c)
+            dn_s.append(s)
+
+        def down_copy(engine, a, tp):
+            grouped = keep.tile([P, 2, P, 4], BF16, name=f"dng{a}{tp}", align_bytes=64)
+            copy_on(
+                engine,
+                grouped[:].rearrange("p t m j -> p m t j"),
+                down_raw[a][:].rearrange("p j (m t) -> p m t j", t=4)[:, :, 2 * tp : 2 * tp + 2, :],
+            )
+            return grouped
+
+        def down_quant(a, tp, grouped):
+            quantise(dn_c[a][:, tp * 256 : tp * 256 + 256], dn_s[a][:, tp * 256 : tp * 256 + 256], grouped[:].rearrange("p t m j -> p (t m j)"))
+
+        def xg_quant(a, half, grouped):
+            cols = slice(half * HALF, (half + 1) * HALF)
+            quantise(xg_c[a][:, cols], xg_s[a][:, cols], grouped[:].rearrange("p c t -> p (c t)"))
+
+        acc = {}
+
+        def w4_pass(a, jc, nh):
+            if a == 0:
+                acc[jc, nh] = psum.tile([P, NT], F32, name=f"bank{jc + 4 * (1 - nh)}")
+            j = slice(jc * P, (jc + 1) * P)
+            nc.tensor.matmul_mx(
+                out=acc[jc, nh][:],
+                lhsT=xg_c[a][:, j].bitcast(E4M3),
+                lhsT_scale=xg_s[a][:, j],
+                rhs=w4w[:, a * 2 * M + nh * 2 * NT : a * 2 * M + (nh + 1) * 2 * NT].bitcast(E2M1),
+                rhs_scale=w4s[:, a * M + nh * NT : a * M + (nh + 1) * NT],
+                start=(a == 0),
+                stop=False,
+            )
+
+        g = [[keep.tile([P, 4, HALF], F32, name=f"g{a}{half}") for half in range(2)] for a in range(PASSES)]
+        dng = [keep.tile([P, 4, P, 4], BF16, name=f"dng{a}", align_bytes=64) for a in range(PASSES)]
+
+        def down_copy(engine, a, mh):
+            m = slice(mh * 64, mh * 64 + 64)
+            copy_on(
+                engine,
+                dng[a][:].rearrange("p t m j -> p m t j")[:, m, :, :],
+                down_raw[a][:].rearrange("p j (m t) -> p m t j", t=4)[:, m, :, :],
+            )
+
+        def down_quant(a, tp):
+            cols = slice(tp * 256, tp * 256 + 256)
+            quantise(dn_c[a][:, cols], dn_s[a][:, cols], dng[a][:].rearrange("p t m j -> p (t m j)")[:, tp * 1024 : tp * 1024 + 1024])
+
+        def down_quant_all(a):
+            quantise(dn_c[a][:], dn_s[a][:], dng[a][:].rearrange("p t m j -> p (t m j)"))
+
+        def xg_copy(engine, a, half):
+            return interleave(engine, f"xgg{a}{half}", g[a][half][:], HALF)
+
+        def gathers(a, i):
+            for half in range(2):
+                gather(a, i, half, g[a])
+
+        def h_chunk(jc, engine):
+            j = slice(jc * P, (jc + 1) * P)
+            bank = psum.tile([P, 4, P], F32, name=f"bank{jc % 2}")
+            for t in range(4):
+                r = slice(t * P, (t + 1) * P)
+                for a in range(PASSES):
+                    nc.tensor.matmul_mx(
+                        out=bank[:, t, :],
+                        lhsT=dn_c[a][:, r].bitcast(E4M3),
+                        lhsT_scale=dn_s[a][:, r],
+                        rhs=xg_c[a][:, j].bitcast(E4M3),
+                        rhs_scale=xg_s[a][:, j],
+                        start=(a == 0),
+                        stop=(a == 1),
+                    )
+            hg = keep.tile([P, P, 4], BF16, name=f"hg{jc}", align_bytes=64)
+            copy_on(engine, hg[:], bank[:].rearrange("p t j -> p j t"))
+            return hg
+
+        h_c = [keep.tile([P, P], U32, name=f"hc{jc}", align_bytes=64) for jc in range(4)]
+        h_s = [keep.tile([P, P], U8, name=f"hs{jc}", align_bytes=64) for jc in range(4)]
+
+        def h_quant(jc, hg):
+            quantise(h_c[jc][:], h_s[jc][:], hg[:].rearrange("p j t -> p (j t)"))
+
+        uc = [keep.tile([P, NT], U32, name=f"uc{nh}", align_bytes=64) for nh in range(2)]
+        us = [keep.tile([P, NT], U8, name=f"us{nh}", align_bytes=64) for nh in range(2)]
+
+        def up_copy(engine, nh, q):
+            return interleave(engine, f"ug{nh}{q}", up_raw[nh][:, :, q * 256 : q * 256 + 256], 256)
+
+        def up_quant(nh, q, grouped):
+            cols = slice(q * 256, q * 256 + 256)
+            quantise(uc[nh][:, cols], us[nh][:, cols], grouped[:].rearrange("p c t -> p (c t)"))
+
+        def mm_pass(jc, nh, which, start, stop):
+            j = slice(jc * P, (jc + 1) * P)
+            if start:
+                acc[jc, nh] = psum.tile([P, NT], F32, name=f"bank{jc + 4 * (1 - nh)}")
+            if which < 2:
+                w = which * M + nh * NT
+                nc.tensor.matmul_mx(
+                    out=acc[jc, nh][:],
+                    lhsT=xg_c[which][:, j].bitcast(E4M3),
+                    lhsT_scale=xg_s[which][:, j],
+                    rhs=w4w[:, 2 * w : 2 * (w + NT)].bitcast(E2M1),
+                    rhs_scale=w4s[:, w : w + NT],
+                    start=start,
+                    stop=stop,
+                )
+            else:
+                nc.tensor.matmul_mx(
+                    out=acc[jc, nh][:],
+                    lhsT=h_c[jc][:].bitcast(E4M3),
+                    lhsT_scale=h_s[jc][:],
+                    rhs=uc[nh][:].bitcast(E4M3),
+                    rhs_scale=us[nh][:],
+                    start=start,
+                    stop=stop,
+                )
+
+        def finish(jc, nh, engine):
+            res = keep.tile([P, NT], F32, name=f"res{jc}{nh}")
+            copy_on(engine, res[:], acc[jc, nh][:])
+            nc.sync.dma_start(out[jc * P : (jc + 1) * P, nh * NT : (nh + 1) * NT], res[:])
+
+        for i in range(4):
+            gathers(0, i)
+        x0 = [xg_copy("S", 0, half) for half in range(2)]
+        for half in range(2):
+            xg_quant(0, half, x0[half])
+        for i in range(4):
+            gathers(1, i)
+        for jc in range(4):
+            mm_pass(jc, 0, 0, True, False)
+        for jc in (2, 3):
+            mm_pass(jc, 1, 0, True, False)
+        x1 = [xg_copy("S", 1, 0), xg_copy("S", 1, 1)]
+        for mh in range(2):
+            down_copy("V", 0, mh)
+        for half in range(2):
+            xg_quant(1, half, x1[half])
+        down_quant_all(0)
+        for mh in range(2):
+            down_copy("S", 1, mh)
+        down_quant_all(1)
+        for jc in range(4):
+            mm_pass(jc, 0, 1, False, False)
+        for jc in (2, 3):
+            mm_pass(jc, 1, 1, False, False)
+        hg = [h_chunk(jc, "SVSV"[jc]) for jc in range(4)]
+        for jc in range(4):
+            h_quant(jc, hg[jc])
+        u0 = [up_copy("V", 0, 0), up_copy("S", 0, 1)]
+        for q in range(2):
+            up_quant(0, q, u0[q])
+        for jc in range(4):
+            mm_pass(jc, 0, 2, False, True)
+            finish(jc, 0, "SVSS"[jc])
+        u1 = [up_copy("V", 1, 0), up_copy("S", 1, 1)]
+        for q in range(2):
+            up_quant(1, q, u1[q])
+        for jc in (0, 1):
+            mm_pass(jc, 1, 0, True, False)
+            mm_pass(jc, 1, 1, False, False)
+        for jc in (2, 3, 0, 1):
+            mm_pass(jc, 1, 2, False, True)
+            finish(jc, 1, "SVSV"[jc])

@@ -32,7 +32,7 @@ def tile_list_hlora_tm_none_kernel(tc, xT, w4_words, w4_scales, down, up, wgt, o
         nc.sync.dma_start(offsets[:], offs)
 
         w4s = keep.tile([P, PASSES * M], U8, name="w4s", align_bytes=64)
-        nc.vector.memset(w4s[:].bitcast(I32), 0)
+        nc.gpsimd.memset(w4s[:].bitcast(I32), 0)
         scale_rows = w4_scales.bitcast(I32).rearrange("a (q r) n -> r q a n", r=4)
 
         wgt_t = keep.tile([P, S], F32, name="wgt_t")
@@ -45,7 +45,7 @@ def tile_list_hlora_tm_none_kernel(tc, xT, w4_words, w4_scales, down, up, wgt, o
         up_raw = [keep.tile([P, 4, NT], F32, name=f"up{nh}") for nh in range(2)]
         w4w = keep.tile([P, PASSES * 2 * M], U8, name="w4w", align_bytes=64)
         w4_view = w4w[:].bitcast(I32).rearrange("p (a n) -> p a n", a=PASSES)
-        for what in ["x00","g00","x01","x02","x03","s00","w00","w10","x10","x11","d00","d01","x12","x13","d10","d11","u00","u10"]:
+        for what in ["x02","g00","s00","x01","x00","x10","x03","x11","D00","x13","x12","w00","D10","u00","u10","w10"]:
             kind, u, v = what[0], int(what[1]), int(what[2])
             if kind == "x":
                 nc.sync.dma_start(planes[u][v][:], x_rows[u, v])
@@ -63,7 +63,7 @@ def tile_list_hlora_tm_none_kernel(tc, xT, w4_words, w4_scales, down, up, wgt, o
                 nc.sync.dma_start(wgt_t[:], wgt)
             if kind == "s":
                 for r in range(4):
-                    nc.sync.dma_start(w4s[r:P:32, :].bitcast(I32).rearrange("q (a n) -> q a n", a=PASSES), scale_rows[r])
+                    nc.gpsimd.dma_start(w4s[r:P:32, :].bitcast(I32).rearrange("q (a n) -> q a n", a=PASSES), scale_rows[r])
 
         def gather(a, i, half, g):
             nc.vector.tensor_tensor(
@@ -104,14 +104,13 @@ def tile_list_hlora_tm_none_kernel(tc, xT, w4_words, w4_scales, down, up, wgt, o
             dn_c.append(c)
             dn_s.append(s)
 
-        def down_copy(engine, a, tp):
-            grouped = keep.tile([P, 2, P, 4], BF16, name=f"dng{a}{tp}", align_bytes=64)
+        def down_copy(engine, a, mh):
+            m = slice(mh * 64, mh * 64 + 64)
             copy_on(
                 engine,
-                grouped[:].rearrange("p t m j -> p m t j"),
-                down_raw[a][:].rearrange("p j (m t) -> p m t j", t=4)[:, :, 2 * tp : 2 * tp + 2, :],
+                dng[a][:].rearrange("p t m j -> p m t j")[:, m, :, :],
+                down_raw[a][:].rearrange("p j (m t) -> p m t j", t=4)[:, m, :, :],
             )
-            return grouped
 
         def down_quant(a, tp, grouped):
             quantise(dn_c[a][:, tp * 256 : tp * 256 + 256], dn_s[a][:, tp * 256 : tp * 256 + 256], grouped[:].rearrange("p t m j -> p (t m j)"))
@@ -139,12 +138,11 @@ def tile_list_hlora_tm_none_kernel(tc, xT, w4_words, w4_scales, down, up, wgt, o
         g = [[keep.tile([P, 4, HALF], F32, name=f"g{a}{half}") for half in range(2)] for a in range(PASSES)]
         dng = [keep.tile([P, 4, P, 4], BF16, name=f"dng{a}", align_bytes=64) for a in range(PASSES)]
 
-        def down_copy(engine, a, mh):
-            m = slice(mh * 64, mh * 64 + 64)
+        def down_copy(engine, a, tp):
             copy_on(
                 engine,
-                dng[a][:].rearrange("p t m j -> p m t j")[:, m, :, :],
-                down_raw[a][:].rearrange("p j (m t) -> p m t j", t=4)[:, m, :, :],
+                dng[a][:].rearrange("p t m j -> p m t j")[:, :, 2 * tp : 2 * tp + 2, :],
+                down_raw[a][:].rearrange("p j (m t) -> p m t j", t=4)[:, :, 2 * tp : 2 * tp + 2, :],
             )
 
         def down_quant(a, tp):
@@ -161,14 +159,17 @@ def tile_list_hlora_tm_none_kernel(tc, xT, w4_words, w4_scales, down, up, wgt, o
             for half in range(2):
                 gather(a, i, half, g[a])
 
-        def h_chunk(jc, engine):
+        hbank = {}
+        hg = [keep.tile([P, P, 4], BF16, name=f"hg{jc}", align_bytes=64) for jc in range(4)]
+
+        def h_mm(jc, n):
             j = slice(jc * P, (jc + 1) * P)
-            bank = psum.tile([P, 4, P], F32, name=f"bank{jc % 2}")
+            hbank[jc] = psum.tile([P, 4, P], F32, name=f"bank{n}")
             for t in range(4):
                 r = slice(t * P, (t + 1) * P)
                 for a in range(PASSES):
                     nc.tensor.matmul_mx(
-                        out=bank[:, t, :],
+                        out=hbank[jc][:, t, :],
                         lhsT=dn_c[a][:, r].bitcast(E4M3),
                         lhsT_scale=dn_s[a][:, r],
                         rhs=xg_c[a][:, j].bitcast(E4M3),
@@ -176,9 +177,9 @@ def tile_list_hlora_tm_none_kernel(tc, xT, w4_words, w4_scales, down, up, wgt, o
                         start=(a == 0),
                         stop=(a == 1),
                     )
-            hg = keep.tile([P, P, 4], BF16, name=f"hg{jc}", align_bytes=64)
-            copy_on(engine, hg[:], bank[:].rearrange("p t j -> p j t"))
-            return hg
+
+        def h_copy(engine, jc):
+            copy_on(engine, hg[jc][:], hbank[jc][:].rearrange("p t j -> p j t"))
 
         h_c = [keep.tile([P, P], U32, name=f"hc{jc}", align_bytes=64) for jc in range(4)]
         h_s = [keep.tile([P, P], U8, name=f"hs{jc}", align_bytes=64) for jc in range(4)]
@@ -222,50 +223,104 @@ def tile_list_hlora_tm_none_kernel(tc, xT, w4_words, w4_scales, down, up, wgt, o
                     stop=stop,
                 )
 
-        def finish(jc, nh, engine):
-            res = keep.tile([P, NT], F32, name=f"res{jc}{nh}")
-            copy_on(engine, res[:], acc[jc, nh][:])
-            nc.sync.dma_start(out[jc * P : (jc + 1) * P, nh * NT : (nh + 1) * NT], res[:])
+        res = {}
 
-        for i in range(4):
-            gathers(0, i)
-        x0 = [xg_copy("S", 0, half) for half in range(2)]
-        for half in range(2):
-            xg_quant(0, half, x0[half])
-        for i in range(4):
-            gathers(1, i)
-        for jc in range(4):
-            mm_pass(jc, 0, 0, True, False)
-        for jc in (2, 3):
-            mm_pass(jc, 1, 0, True, False)
-        x1 = [xg_copy("S", 1, 0), xg_copy("S", 1, 1)]
-        for mh in range(2):
-            down_copy("V", 0, mh)
-        for half in range(2):
-            xg_quant(1, half, x1[half])
+        def finish(jc, nh, engine):
+            res[jc, nh] = keep.tile([P, NT], F32, name=f"res{jc}{nh}")
+            copy_on(engine, res[jc, nh][:], acc[jc, nh][:])
+
+        def store(jc, nh):
+            nc.sync.dma_start(out[jc * P : (jc + 1) * P, nh * NT : (nh + 1) * NT], res[jc, nh][:])
+
+        xgg = {}
+        ug = {}
+        gather(0, 2, 0, g[0])
+        gather(0, 1, 0, g[0])
+        gather(0, 0, 0, g[0])
+        gather(0, 3, 0, g[0])
+        xgg[0, 0] = xg_copy("S", 0, 0)
+        down_copy("S", 1, 1)
+        gather(1, 0, 0, g[1])
+        down_copy("S", 0, 0)
+        down_copy("S", 0, 1)
+        gather(1, 1, 0, g[1])
+        gather(1, 2, 0, g[1])
+        gather(1, 3, 0, g[1])
+        xgg[1, 0] = xg_copy("S", 1, 0)
+        down_copy("V", 1, 0)
         down_quant_all(0)
-        for mh in range(2):
-            down_copy("S", 1, mh)
         down_quant_all(1)
-        for jc in range(4):
-            mm_pass(jc, 0, 1, False, False)
-        for jc in (2, 3):
-            mm_pass(jc, 1, 1, False, False)
-        hg = [h_chunk(jc, "SVSV"[jc]) for jc in range(4)]
-        for jc in range(4):
-            h_quant(jc, hg[jc])
-        u0 = [up_copy("V", 0, 0), up_copy("S", 0, 1)]
-        for q in range(2):
-            up_quant(0, q, u0[q])
-        for jc in range(4):
-            mm_pass(jc, 0, 2, False, True)
-            finish(jc, 0, "SVSS"[jc])
-        u1 = [up_copy("V", 1, 0), up_copy("S", 1, 1)]
-        for q in range(2):
-            up_quant(1, q, u1[q])
-        for jc in (0, 1):
-            mm_pass(jc, 1, 0, True, False)
-            mm_pass(jc, 1, 1, False, False)
-        for jc in (2, 3, 0, 1):
-            mm_pass(jc, 1, 2, False, True)
-            finish(jc, 1, "SVSV"[jc])
+        xg_quant(0, 0, xgg[0, 0])
+        xg_quant(1, 0, xgg[1, 0])
+        h_mm(1, 1 % 2)
+        gather(0, 0, 1, g[0])
+        gather(0, 1, 1, g[0])
+        gather(0, 2, 1, g[0])
+        gather(0, 3, 1, g[0])
+        xgg[0, 1] = xg_copy("S", 0, 1)
+        xg_quant(0, 1, xgg[0, 1])
+        gather(1, 2, 1, g[1])
+        ug[0, 0] = up_copy("V", 0, 0)
+        gather(1, 0, 1, g[1])
+        gather(1, 1, 1, g[1])
+        gather(1, 3, 1, g[1])
+        xgg[1, 1] = xg_copy("V", 1, 1)
+        h_copy("S", 1)
+        xg_quant(1, 1, xgg[1, 1])
+        h_mm(3, 3 % 2)
+        ug[0, 1] = up_copy("V", 0, 1)
+        h_copy("S", 3)
+        mm_pass(3, 0, 0, True, False)
+        up_quant(0, 1, ug[0, 1])
+        h_quant(3, hg[3])
+        up_quant(0, 0, ug[0, 0])
+        mm_pass(3, 0, 2, False, False)
+        mm_pass(3, 0, 1, False, True)
+        h_mm(0, 0 % 2)
+        finish(3, 0, "S")
+        h_copy("S", 0)
+        h_quant(0, hg[0])
+        mm_pass(0, 0, 2, True, False)
+        store(3, 0)
+        h_mm(2, 2 % 2)
+        ug[1, 0] = up_copy("V", 1, 0)
+        h_quant(1, hg[1])
+        h_copy("S", 2)
+        ug[1, 1] = up_copy("V", 1, 1)
+        h_quant(2, hg[2])
+        mm_pass(1, 0, 0, True, False)
+        mm_pass(2, 0, 2, True, False)
+        mm_pass(1, 0, 1, False, False)
+        mm_pass(1, 0, 2, False, True)
+        mm_pass(0, 0, 1, False, False)
+        finish(1, 0, "S")
+        store(1, 0)
+        up_quant(1, 0, ug[1, 0])
+        mm_pass(2, 0, 1, False, False)
+        mm_pass(0, 0, 0, False, True)
+        up_quant(1, 1, ug[1, 1])
+        finish(0, 0, "S")
+        mm_pass(1, 1, 1, True, False)
+        mm_pass(1, 1, 2, False, False)
+        mm_pass(3, 1, 0, True, False)
+        mm_pass(3, 1, 1, False, False)
+        mm_pass(3, 1, 2, False, True)
+        mm_pass(2, 0, 0, False, True)
+        finish(3, 1, "V")
+        finish(2, 0, "V")
+        mm_pass(2, 1, 1, True, False)
+        mm_pass(1, 1, 0, False, True)
+        store(0, 0)
+        finish(1, 1, "S")
+        store(3, 1)
+        mm_pass(0, 1, 1, True, False)
+        store(1, 1)
+        mm_pass(0, 1, 0, False, False)
+        mm_pass(0, 1, 2, False, True)
+        mm_pass(2, 1, 0, False, False)
+        mm_pass(2, 1, 2, False, True)
+        finish(0, 1, "S")
+        finish(2, 1, "V")
+        store(2, 0)
+        store(0, 1)
+        store(2, 1)

@@ -45,7 +45,7 @@ def tile_list_hlora_tm_none_kernel(tc, xT, w4_words, w4_scales, down, up, wgt, o
         up_raw = [keep.tile([P, 4, NT], F32, name=f"up{nh}") for nh in range(2)]
         w4w = keep.tile([P, PASSES * 2 * M], U8, name="w4w", align_bytes=64)
         w4_view = w4w[:].bitcast(I32).rearrange("p (a n) -> p a n", a=PASSES)
-        for what in ["x02","g00","s00","x01","x00","x10","x03","x11","D00","x13","x12","w00","D10","u00","u10","w10"]:
+        for what in ["s00","g00","x11","x10","x03","x01","x12","x13","x00","x02","D10","w00","D00","u00","u10","w10"]:
             kind, u, v = what[0], int(what[1]), int(what[2])
             if kind == "x":
                 nc.sync.dma_start(planes[u][v][:], x_rows[u, v])
@@ -63,7 +63,7 @@ def tile_list_hlora_tm_none_kernel(tc, xT, w4_words, w4_scales, down, up, wgt, o
                 nc.sync.dma_start(wgt_t[:], wgt)
             if kind == "s":
                 for r in range(4):
-                    nc.gpsimd.dma_start(w4s[r:P:32, :].bitcast(I32).rearrange("q (a n) -> q a n", a=PASSES), scale_rows[r])
+                    nc.scalar.dma_start(w4s[r:P:32, :].bitcast(I32).rearrange("q (a n) -> q a n", a=PASSES), scale_rows[r])
 
         def gather(a, i, half, g):
             nc.vector.tensor_tensor(
@@ -81,11 +81,10 @@ def tile_list_hlora_tm_none_kernel(tc, xT, w4_words, w4_scales, down, up, wgt, o
 
         def interleave(engine, name, src, width):
             grouped = keep.tile([P, width, 4], BF16, name=name, align_bytes=64)
-            copy_on(
-                engine,
-                grouped[:].rearrange("p (c i) t -> p c t i", i=4),
-                src.rearrange("p t (c i) -> p c t i", i=4),
-            )
+            if engine == "S":
+                nc.scalar.copy(grouped[:].rearrange("p (c i) t -> p c t i", i=4), src.rearrange("p t (c i) -> p c t i", i=4))
+            else:
+                nc.vector.tensor_copy(grouped[:], src.rearrange("p t c -> p c t"))
             return grouped
 
         def quantise(codes, scales, grouped):
@@ -106,11 +105,10 @@ def tile_list_hlora_tm_none_kernel(tc, xT, w4_words, w4_scales, down, up, wgt, o
 
         def down_copy(engine, a, mh):
             m = slice(mh * 64, mh * 64 + 64)
-            copy_on(
-                engine,
-                dng[a][:].rearrange("p t m j -> p m t j")[:, m, :, :],
-                down_raw[a][:].rearrange("p j (m t) -> p m t j", t=4)[:, m, :, :],
-            )
+            if engine == "S":
+                nc.scalar.copy(dng[a][:].rearrange("p t m j -> p m t j")[:, m, :, :], down_raw[a][:].rearrange("p j (m t) -> p m t j", t=4)[:, m, :, :])
+            else:
+                nc.vector.tensor_copy(dng[a][:, :, m, :], down_raw[a][:].rearrange("p j (m t) -> p t m j", t=4)[:, :, m, :])
 
         def down_quant(a, tp, grouped):
             quantise(dn_c[a][:, tp * 256 : tp * 256 + 256], dn_s[a][:, tp * 256 : tp * 256 + 256], grouped[:].rearrange("p t m j -> p (t m j)"))
@@ -234,93 +232,93 @@ def tile_list_hlora_tm_none_kernel(tc, xT, w4_words, w4_scales, down, up, wgt, o
 
         xgg = {}
         ug = {}
-        gather(0, 2, 0, g[0])
-        gather(0, 1, 0, g[0])
-        gather(0, 0, 0, g[0])
+        gather(1, 2, 0, g[1])
         gather(0, 3, 0, g[0])
-        xgg[0, 0] = xg_copy("S", 0, 0)
-        down_copy("S", 1, 1)
+        down_copy("S", 1, 0)
         gather(1, 0, 0, g[1])
         down_copy("S", 0, 0)
-        down_copy("S", 0, 1)
-        gather(1, 1, 0, g[1])
-        gather(1, 2, 0, g[1])
+        down_copy("V", 1, 1)
+        gather(0, 1, 0, g[0])
         gather(1, 3, 0, g[1])
+        gather(1, 1, 0, g[1])
+        gather(0, 0, 0, g[0])
+        gather(0, 2, 0, g[0])
         xgg[1, 0] = xg_copy("S", 1, 0)
-        down_copy("V", 1, 0)
-        down_quant_all(0)
+        down_copy("V", 0, 1)
+        xgg[0, 0] = xg_copy("S", 0, 0)
         down_quant_all(1)
+        down_quant_all(0)
         xg_quant(0, 0, xgg[0, 0])
         xg_quant(1, 0, xgg[1, 0])
-        h_mm(1, 1 % 2)
+        h_mm(0, 0 % 2)
+        h_copy("V", 0)
+        gather(1, 1, 1, g[1])
+        ug[0, 1] = up_copy("S", 0, 1)
         gather(0, 0, 1, g[0])
+        gather(1, 3, 1, g[1])
         gather(0, 1, 1, g[0])
         gather(0, 2, 1, g[0])
         gather(0, 3, 1, g[0])
         xgg[0, 1] = xg_copy("S", 0, 1)
-        xg_quant(0, 1, xgg[0, 1])
-        gather(1, 2, 1, g[1])
-        ug[0, 0] = up_copy("V", 0, 0)
         gather(1, 0, 1, g[1])
-        gather(1, 1, 1, g[1])
-        gather(1, 3, 1, g[1])
-        xgg[1, 1] = xg_copy("V", 1, 1)
-        h_copy("S", 1)
+        gather(1, 2, 1, g[1])
+        xgg[1, 1] = xg_copy("S", 1, 1)
+        xg_quant(0, 1, xgg[0, 1])
+        mm_pass(2, 0, 0, True, False)
         xg_quant(1, 1, xgg[1, 1])
-        h_mm(3, 3 % 2)
-        ug[0, 1] = up_copy("V", 0, 1)
-        h_copy("S", 3)
-        mm_pass(3, 0, 0, True, False)
+        h_mm(2, 2 % 2)
         up_quant(0, 1, ug[0, 1])
-        h_quant(3, hg[3])
+        ug[0, 0] = up_copy("V", 0, 0)
+        mm_pass(2, 0, 1, False, False)
+        h_copy("S", 2)
         up_quant(0, 0, ug[0, 0])
-        mm_pass(3, 0, 2, False, False)
-        mm_pass(3, 0, 1, False, True)
-        h_mm(0, 0 % 2)
-        finish(3, 0, "S")
-        h_copy("S", 0)
+        h_quant(2, hg[2])
+        mm_pass(2, 0, 2, False, True)
+        finish(2, 0, "V")
         h_quant(0, hg[0])
         mm_pass(0, 0, 2, True, False)
-        store(3, 0)
-        h_mm(2, 2 % 2)
-        ug[1, 0] = up_copy("V", 1, 0)
+        mm_pass(3, 1, 1, True, False)
+        h_mm(1, 1 % 2)
+        h_copy("S", 1)
+        mm_pass(2, 1, 1, True, False)
         h_quant(1, hg[1])
-        h_copy("S", 2)
-        ug[1, 1] = up_copy("V", 1, 1)
-        h_quant(2, hg[2])
         mm_pass(1, 0, 0, True, False)
-        mm_pass(2, 0, 2, True, False)
         mm_pass(1, 0, 1, False, False)
         mm_pass(1, 0, 2, False, True)
-        mm_pass(0, 0, 1, False, False)
         finish(1, 0, "S")
-        store(1, 0)
+        ug[1, 0] = up_copy("V", 1, 0)
+        ug[1, 1] = up_copy("V", 1, 1)
         up_quant(1, 0, ug[1, 0])
-        mm_pass(2, 0, 1, False, False)
-        mm_pass(0, 0, 0, False, True)
         up_quant(1, 1, ug[1, 1])
-        finish(0, 0, "S")
-        mm_pass(1, 1, 1, True, False)
-        mm_pass(1, 1, 2, False, False)
-        mm_pass(3, 1, 0, True, False)
-        mm_pass(3, 1, 1, False, False)
-        mm_pass(3, 1, 2, False, True)
-        mm_pass(2, 0, 0, False, True)
-        finish(3, 1, "V")
-        finish(2, 0, "V")
-        mm_pass(2, 1, 1, True, False)
-        mm_pass(1, 1, 0, False, True)
-        store(0, 0)
-        finish(1, 1, "S")
-        store(3, 1)
-        mm_pass(0, 1, 1, True, False)
-        store(1, 1)
-        mm_pass(0, 1, 0, False, False)
-        mm_pass(0, 1, 2, False, True)
-        mm_pass(2, 1, 0, False, False)
-        mm_pass(2, 1, 2, False, True)
-        finish(0, 1, "S")
-        finish(2, 1, "V")
-        store(2, 0)
-        store(0, 1)
+        mm_pass(2, 1, 2, False, False)
+        mm_pass(2, 1, 0, False, True)
+        finish(2, 1, "S")
+        h_mm(3, 3 % 2)
+        mm_pass(0, 1, 2, True, False)
+        mm_pass(0, 1, 1, False, False)
+        mm_pass(0, 1, 0, False, True)
+        finish(0, 1, "V")
+        h_copy("S", 3)
+        h_quant(3, hg[3])
+        mm_pass(3, 0, 0, True, False)
         store(2, 1)
+        mm_pass(3, 1, 2, False, False)
+        mm_pass(3, 1, 0, False, True)
+        finish(3, 1, "V")
+        mm_pass(0, 0, 1, False, False)
+        store(3, 1)
+        store(1, 0)
+        mm_pass(0, 0, 0, False, True)
+        mm_pass(3, 0, 1, False, False)
+        mm_pass(3, 0, 2, False, True)
+        mm_pass(1, 1, 1, True, False)
+        finish(0, 0, "S")
+        finish(3, 0, "S")
+        mm_pass(1, 1, 0, False, False)
+        mm_pass(1, 1, 2, False, True)
+        store(0, 1)
+        finish(1, 1, "S")
+        store(0, 0)
+        store(2, 0)
+        store(3, 0)
+        store(1, 1)

@@ -16,309 +16,225 @@ E2M1 = mybir.dt.float4_e2m1fn_x4
 MULT = mybir.AluOpType.mult
 
 P = 128
-PASSES = K // 512
-HALF = S // 2
-NT = 512
+I4 = 4
+PASSES = K // (P * I4)
+LIST_HALF = S // 2
+N_HALF = M // 2
+COPY_COLUMNS = 256
+R_HALF = R // 2
+J_TILES = S // P
 
 
 def tile_list_hlora_tm_none_kernel(tc, xT, w4_words, w4_scales, down, up, wgt, offs, out):
     nc = tc.nc
     with ExitStack() as ctx:
-        held = ctx.enter_context(tc.tile_pool(name="held", bufs=1))
+        lists = ctx.enter_context(tc.tile_pool(name="lists", bufs=1))
         keep = ctx.enter_context(tc.tile_pool(name="keep", bufs=1))
         psum = ctx.enter_context(tc.psum_pool(name="psum", bufs=1))
 
-        offsets = held.tile([P, S // 16], U16, name="offsets")
+        offsets = lists.tile([P, S // 16], U16, name="offsets")
         nc.sync.dma_start(offsets[:], offs)
 
-        w4s = keep.tile([P, PASSES * M], U8, name="w4s", align_bytes=64)
-        nc.gpsimd.memset(w4s[:].bitcast(I32), 0)
-        scale_rows = w4_scales.bitcast(I32).rearrange("a (q r) n -> r q a n", r=4)
+        w4_scale = keep.tile([P, PASSES * M], U8, name="w4_scale", align_bytes=64)
+        nc.gpsimd.memset(w4_scale[:].bitcast(I32), 0)
 
-        wgt_t = keep.tile([P, S], F32, name="wgt_t")
-        x_rows = xT.rearrange("(a p i) t -> a i p t", a=PASSES, i=4)
-        down_rows = down.rearrange("(a p i) r -> a p i r", a=PASSES, i=4)
-        up_rows = up.rearrange("(p i) n -> p i n", i=4)
-        w4_rows = w4_words.bitcast(I32).rearrange("a p n -> p a n")
-        planes = [[keep.tile([P, T], F32, name=f"x{a}{i}") for i in range(4)] for a in range(PASSES)]
-        down_raw = [keep.tile([P, 4, R], F32, name=f"down{a}") for a in range(PASSES)]
-        up_raw = [keep.tile([P, 4, NT], F32, name=f"up{nh}") for nh in range(2)]
-        w4w = keep.tile([P, PASSES * 2 * M], U8, name="w4w", align_bytes=64)
-        w4_view = w4w[:].bitcast(I32).rearrange("p (a n) -> p a n", a=PASSES)
-        for what in ["s00","g00","x11","x10","x03","x01","x12","x13","x00","x02","D10","w00","D00","u00","u10","w10"]:
-            kind, u, v = what[0], int(what[1]), int(what[2])
-            if kind == "x":
-                nc.sync.dma_start(planes[u][v][:], x_rows[u, v])
-            if kind == "d":
-                nc.sync.dma_start(down_raw[u][:, :, v * 256 : v * 256 + 256], down_rows[u][:, :, v * 256 : v * 256 + 256])
-            if kind == "D":
-                nc.sync.dma_start(down_raw[u][:], down_rows[u])
-            if kind == "u":
-                nc.sync.dma_start(up_raw[u][:], up_rows[:, :, u * NT : (u + 1) * NT])
-            if kind == "w":
-                nc.sync.dma_start(w4_view[:, :, u * 256 : u * 256 + 256], w4_rows[:, :, u * 256 : u * 256 + 256])
-            if kind == "W":
-                nc.sync.dma_start(w4_view, w4_rows)
-            if kind == "g":
-                nc.sync.dma_start(wgt_t[:], wgt)
-            if kind == "s":
-                for r in range(4):
-                    nc.scalar.dma_start(w4s[r:P:32, :].bitcast(I32).rearrange("q (a n) -> q a n", a=PASSES), scale_rows[r])
+        wgt_sb = keep.tile([P, S], F32, name="wgt_sb")
+        planes = [[keep.tile([P, T], F32, name=f"plane{a}{i}") for i in range(I4)] for a in range(PASSES)]
+        down_raw = [keep.tile([P, I4, R], F32, name=f"down_raw{a}") for a in range(PASSES)]
+        up_raw = [keep.tile([P, I4, N_HALF], F32, name=f"up_raw{nh}") for nh in range(2)]
+        w4_word = keep.tile([P, PASSES * 2 * M], U8, name="w4_word", align_bytes=64)
 
-        def gather(a, i, half, g):
-            nc.vector.tensor_tensor(
-                g[half][:, i, :],
-                planes[a][i][:].indirect(offsets[:, half * 16 : half * 16 + 16]),
-                wgt_t[:, half * HALF : (half + 1) * HALF],
-                MULT,
+        x_rows = xT.rearrange("(a p i) t -> a i p t", a=PASSES, i=I4)
+        down_rows = down.rearrange("(a p i) r -> a p i r", a=PASSES, i=I4)
+        up_rows = up.rearrange("(p i) n -> p i n", i=I4)
+        scale_rows = w4_scales.bitcast(I32).rearrange("a (q s) n -> s q a n", s=4)
+
+        def load_plane(a, i):
+            nc.sync.dma_start(planes[a][i][:], x_rows[a, i])
+
+        def load_w4_scales():
+            for s in range(4):
+                rows = w4_scale[s:P:32, :].bitcast(I32)
+                nc.sync.dma_start(rows.rearrange("q (a n) -> q a n", a=PASSES), scale_rows[s])
+
+        load_plane(0, 0)
+        nc.sync.dma_start(wgt_sb[:], wgt)
+        for i in range(1, I4):
+            load_plane(0, i)
+        load_plane(1, 0)
+        load_w4_scales()
+        load_plane(1, 1)
+        nc.sync.dma_start(down_raw[0][:], down_rows[0])
+        load_plane(1, 2)
+        load_plane(1, 3)
+        nc.sync.dma_start(
+            w4_word[:].bitcast(I32).rearrange("p (a n) -> p a n", a=PASSES),
+            w4_words.bitcast(I32).rearrange("a p n -> p a n"),
+        )
+        nc.sync.dma_start(down_raw[1][:], down_rows[1])
+        for nh in range(2):
+            nc.sync.dma_start(up_raw[nh][:], up_rows[:, :, nh * N_HALF : (nh + 1) * N_HALF])
+
+        xg_code, xg_scale, down_code, down_scale = [], [], [], []
+        for a in range(PASSES):
+            xg_code.append(keep.tile([P, S], U32, name=f"xg_code{a}", align_bytes=64))
+            xg_scale.append(keep.tile([P, S], U8, name=f"xg_scale{a}", align_bytes=64))
+        for a in range(PASSES):
+            down_code.append(keep.tile([P, R], U32, name=f"down_code{a}", align_bytes=64))
+            down_scale.append(keep.tile([P, R], U8, name=f"down_scale{a}", align_bytes=64))
+        picked = [[keep.tile([P, I4, LIST_HALF], F32, name=f"picked{a}{half}") for half in range(2)] for a in range(PASSES)]
+        down_bf = [keep.tile([P, I4, P, I4], BF16, name=f"down_bf{a}", align_bytes=64) for a in range(PASSES)]
+        h_bf = [keep.tile([P, P, I4], BF16, name=f"h_bf{jt}", align_bytes=64) for jt in range(J_TILES)]
+        h_code = [keep.tile([P, P], U32, name=f"h_code{jt}", align_bytes=64) for jt in range(J_TILES)]
+        h_scale = [keep.tile([P, P], U8, name=f"h_scale{jt}", align_bytes=64) for jt in range(J_TILES)]
+        up_code = [keep.tile([P, N_HALF], U32, name=f"up_code{nh}", align_bytes=64) for nh in range(2)]
+        up_scale = [keep.tile([P, N_HALF], U8, name=f"up_scale{nh}", align_bytes=64) for nh in range(2)]
+        xg_bf, up_bf, h_sum, out_sum = {}, {}, {}, {}
+
+        def quantise(code, scale, values):
+            nc.vector.quantize_mx(out=code.bitcast(E4M3), scales=scale, in_=values)
+
+        def interleave(copy, dst, src):
+            copy(dst.rearrange("p (c e) i -> p c i e", e=4), src.rearrange("p i (c e) -> p c i e", e=4))
+
+        def gather(a, i):
+            for half in range(2):
+                nc.vector.tensor_tensor(
+                    picked[a][half][:, i, :],
+                    planes[a][i][:].indirect(offsets[:, half * LIST_HALF // 16 : (half + 1) * LIST_HALF // 16]),
+                    wgt_sb[:, half * LIST_HALF : (half + 1) * LIST_HALF],
+                    MULT,
+                )
+
+        def copy_xg(copy, a, half):
+            xg_bf[a, half] = keep.tile([P, LIST_HALF, I4], BF16, name=f"xg_bf{a}{half}", align_bytes=64)
+            interleave(copy, xg_bf[a, half][:], picked[a][half][:])
+
+        def quantise_xg(a, half):
+            cols = slice(half * LIST_HALF, (half + 1) * LIST_HALF)
+            quantise(xg_code[a][:, cols], xg_scale[a][:, cols], xg_bf[a, half][:].rearrange("p c i -> p (c i)"))
+
+        def copy_down(copy, a, half):
+            m = slice(half * R_HALF // I4, (half + 1) * R_HALF // I4)
+            copy(
+                down_bf[a][:].rearrange("p t m i -> p m t i")[:, m, :, :],
+                down_raw[a][:].rearrange("p i (m t) -> p m t i", t=I4)[:, m, :, :],
             )
 
-        def copy_on(engine, dst, src):
-            if engine == "S":
-                nc.scalar.copy(dst, src)
-            else:
-                nc.vector.tensor_copy(dst, src)
+        def quantise_down(a):
+            quantise(down_code[a][:], down_scale[a][:], down_bf[a][:].rearrange("p t m i -> p (t m i)"))
 
-        def interleave(engine, name, src, width):
-            grouped = keep.tile([P, width, 4], BF16, name=name, align_bytes=64)
-            if engine == "S":
-                nc.scalar.copy(grouped[:].rearrange("p (c i) t -> p c t i", i=4), src.rearrange("p t (c i) -> p c t i", i=4))
-            else:
-                nc.vector.tensor_copy(grouped[:], src.rearrange("p t c -> p c t"))
-            return grouped
+        def multiply_h(jt):
+            j = slice(jt * P, (jt + 1) * P)
+            h_sum[jt] = psum.tile([P, I4, P], F32, name=f"bank{jt % 2}")
+            for t in range(I4):
+                cols = slice(t * P, (t + 1) * P)
+                for a in range(PASSES):
+                    nc.tensor.matmul_mx(
+                        out=h_sum[jt][:, t, :],
+                        lhsT=down_code[a][:, cols].bitcast(E4M3),
+                        lhsT_scale=down_scale[a][:, cols],
+                        rhs=xg_code[a][:, j].bitcast(E4M3),
+                        rhs_scale=xg_scale[a][:, j],
+                        start=(a == 0),
+                        stop=(a == PASSES - 1),
+                    )
 
-        def quantise(codes, scales, grouped):
-            nc.vector.quantize_mx(out=codes.bitcast(E4M3), scales=scales, in_=grouped)
+        def copy_h(copy, jt):
+            copy(h_bf[jt][:], h_sum[jt][:].rearrange("p t j -> p j t"))
 
-        xg_c, xg_s = [], []
-        for a in range(PASSES):
-            c = keep.tile([P, S], U32, name=f"xgc{a}", align_bytes=64)
-            s = keep.tile([P, S], U8, name=f"xgs{a}", align_bytes=64)
-            xg_c.append(c)
-            xg_s.append(s)
-        dn_c, dn_s = [], []
-        for a in range(PASSES):
-            c = keep.tile([P, R], U32, name=f"dnc{a}", align_bytes=64)
-            s = keep.tile([P, R], U8, name=f"dns{a}", align_bytes=64)
-            dn_c.append(c)
-            dn_s.append(s)
+        def quantise_h(jt):
+            quantise(h_code[jt][:], h_scale[jt][:], h_bf[jt][:].rearrange("p j t -> p (j t)"))
 
-        def down_copy(engine, a, mh):
-            m = slice(mh * 64, mh * 64 + 64)
-            if engine == "S":
-                nc.scalar.copy(dng[a][:].rearrange("p t m j -> p m t j")[:, m, :, :], down_raw[a][:].rearrange("p j (m t) -> p m t j", t=4)[:, m, :, :])
-            else:
-                nc.vector.tensor_copy(dng[a][:, :, m, :], down_raw[a][:].rearrange("p j (m t) -> p t m j", t=4)[:, :, m, :])
+        def copy_up(copy, nh, part):
+            up_bf[nh, part] = keep.tile([P, COPY_COLUMNS, I4], BF16, name=f"up_bf{nh}{part}", align_bytes=64)
+            interleave(copy, up_bf[nh, part][:], up_raw[nh][:, :, part * COPY_COLUMNS : (part + 1) * COPY_COLUMNS])
 
-        def down_quant(a, tp, grouped):
-            quantise(dn_c[a][:, tp * 256 : tp * 256 + 256], dn_s[a][:, tp * 256 : tp * 256 + 256], grouped[:].rearrange("p t m j -> p (t m j)"))
+        def quantise_up(nh, part):
+            cols = slice(part * COPY_COLUMNS, (part + 1) * COPY_COLUMNS)
+            quantise(up_code[nh][:, cols], up_scale[nh][:, cols], up_bf[nh, part][:].rearrange("p c i -> p (c i)"))
 
-        def xg_quant(a, half, grouped):
-            cols = slice(half * HALF, (half + 1) * HALF)
-            quantise(xg_c[a][:, cols], xg_s[a][:, cols], grouped[:].rearrange("p c t -> p (c t)"))
-
-        acc = {}
-
-        def w4_pass(a, jc, nh):
+        def multiply_w4(a, jt, nh):
             if a == 0:
-                acc[jc, nh] = psum.tile([P, NT], F32, name=f"bank{jc + 4 * (1 - nh)}")
-            j = slice(jc * P, (jc + 1) * P)
+                out_sum[jt, nh] = psum.tile([P, N_HALF], F32, name=f"bank{jt + J_TILES * (1 - nh)}")
+            j = slice(jt * P, (jt + 1) * P)
+            w = a * M + nh * N_HALF
             nc.tensor.matmul_mx(
-                out=acc[jc, nh][:],
-                lhsT=xg_c[a][:, j].bitcast(E4M3),
-                lhsT_scale=xg_s[a][:, j],
-                rhs=w4w[:, a * 2 * M + nh * 2 * NT : a * 2 * M + (nh + 1) * 2 * NT].bitcast(E2M1),
-                rhs_scale=w4s[:, a * M + nh * NT : a * M + (nh + 1) * NT],
+                out=out_sum[jt, nh][:],
+                lhsT=xg_code[a][:, j].bitcast(E4M3),
+                lhsT_scale=xg_scale[a][:, j],
+                rhs=w4_word[:, 2 * w : 2 * (w + N_HALF)].bitcast(E2M1),
+                rhs_scale=w4_scale[:, w : w + N_HALF],
                 start=(a == 0),
                 stop=False,
             )
 
-        g = [[keep.tile([P, 4, HALF], F32, name=f"g{a}{half}") for half in range(2)] for a in range(PASSES)]
-        dng = [keep.tile([P, 4, P, 4], BF16, name=f"dng{a}", align_bytes=64) for a in range(PASSES)]
-
-        def down_copy(engine, a, tp):
-            copy_on(
-                engine,
-                dng[a][:].rearrange("p t m j -> p m t j")[:, :, 2 * tp : 2 * tp + 2, :],
-                down_raw[a][:].rearrange("p j (m t) -> p m t j", t=4)[:, :, 2 * tp : 2 * tp + 2, :],
+        def multiply_up(jt, nh):
+            nc.tensor.matmul_mx(
+                out=out_sum[jt, nh][:],
+                lhsT=h_code[jt][:].bitcast(E4M3),
+                lhsT_scale=h_scale[jt][:],
+                rhs=up_code[nh][:].bitcast(E4M3),
+                rhs_scale=up_scale[nh][:],
+                start=False,
+                stop=True,
             )
 
-        def down_quant(a, tp):
-            cols = slice(tp * 256, tp * 256 + 256)
-            quantise(dn_c[a][:, cols], dn_s[a][:, cols], dng[a][:].rearrange("p t m j -> p (t m j)")[:, tp * 1024 : tp * 1024 + 1024])
+        def finish(copy, jt, nh):
+            result = keep.tile([P, N_HALF], F32, name=f"result{jt}{nh}")
+            copy(result[:], out_sum[jt, nh][:])
+            nc.sync.dma_start(out[jt * P : (jt + 1) * P, nh * N_HALF : (nh + 1) * N_HALF], result[:])
 
-        def down_quant_all(a):
-            quantise(dn_c[a][:], dn_s[a][:], dng[a][:].rearrange("p t m j -> p (t m j)"))
+        scalar, vector = nc.scalar.copy, nc.vector.tensor_copy
 
-        def xg_copy(engine, a, half):
-            return interleave(engine, f"xgg{a}{half}", g[a][half][:], HALF)
+        for i in range(I4):
+            gather(0, i)
+        for half in range(2):
+            copy_xg(scalar, 0, half)
+        gather(1, 0)
+        gather(1, 1)
+        for half in range(2):
+            quantise_xg(0, half)
+        for half in range(2):
+            copy_down(scalar, 0, half)
+        for jt in range(J_TILES):
+            multiply_w4(0, jt, 0)
+        gather(1, 2)
+        gather(1, 3)
+        quantise_down(0)
+        copy_xg(scalar, 1, 0)
+        copy_xg(vector, 1, 1)
+        copy_down(scalar, 1, 0)
+        copy_down(vector, 1, 1)
+        for half in range(2):
+            quantise_xg(1, half)
+        quantise_down(1)
+        for jt in range(J_TILES):
+            multiply_w4(1, jt, 0)
 
-        def gathers(a, i):
-            for half in range(2):
-                gather(a, i, half, g[a])
+        for jt in range(J_TILES):
+            multiply_h(jt)
+            copy_h(scalar, jt)
+            quantise_h(jt)
 
-        hbank = {}
-        hg = [keep.tile([P, P, 4], BF16, name=f"hg{jc}", align_bytes=64) for jc in range(4)]
+        for part in range(2):
+            copy_up(vector, 0, part)
+        for part in range(2):
+            quantise_up(0, part)
+        for jt in range(J_TILES):
+            multiply_up(jt, 0)
+            finish(scalar, jt, 0)
 
-        def h_mm(jc, n):
-            j = slice(jc * P, (jc + 1) * P)
-            hbank[jc] = psum.tile([P, 4, P], F32, name=f"bank{n}")
-            for t in range(4):
-                r = slice(t * P, (t + 1) * P)
-                for a in range(PASSES):
-                    nc.tensor.matmul_mx(
-                        out=hbank[jc][:, t, :],
-                        lhsT=dn_c[a][:, r].bitcast(E4M3),
-                        lhsT_scale=dn_s[a][:, r],
-                        rhs=xg_c[a][:, j].bitcast(E4M3),
-                        rhs_scale=xg_s[a][:, j],
-                        start=(a == 0),
-                        stop=(a == 1),
-                    )
-
-        def h_copy(engine, jc):
-            copy_on(engine, hg[jc][:], hbank[jc][:].rearrange("p t j -> p j t"))
-
-        h_c = [keep.tile([P, P], U32, name=f"hc{jc}", align_bytes=64) for jc in range(4)]
-        h_s = [keep.tile([P, P], U8, name=f"hs{jc}", align_bytes=64) for jc in range(4)]
-
-        def h_quant(jc, hg):
-            quantise(h_c[jc][:], h_s[jc][:], hg[:].rearrange("p j t -> p (j t)"))
-
-        uc = [keep.tile([P, NT], U32, name=f"uc{nh}", align_bytes=64) for nh in range(2)]
-        us = [keep.tile([P, NT], U8, name=f"us{nh}", align_bytes=64) for nh in range(2)]
-
-        def up_copy(engine, nh, q):
-            return interleave(engine, f"ug{nh}{q}", up_raw[nh][:, :, q * 256 : q * 256 + 256], 256)
-
-        def up_quant(nh, q, grouped):
-            cols = slice(q * 256, q * 256 + 256)
-            quantise(uc[nh][:, cols], us[nh][:, cols], grouped[:].rearrange("p c t -> p (c t)"))
-
-        def mm_pass(jc, nh, which, start, stop):
-            j = slice(jc * P, (jc + 1) * P)
-            if start:
-                acc[jc, nh] = psum.tile([P, NT], F32, name=f"bank{jc + 4 * (1 - nh)}")
-            if which < 2:
-                w = which * M + nh * NT
-                nc.tensor.matmul_mx(
-                    out=acc[jc, nh][:],
-                    lhsT=xg_c[which][:, j].bitcast(E4M3),
-                    lhsT_scale=xg_s[which][:, j],
-                    rhs=w4w[:, 2 * w : 2 * (w + NT)].bitcast(E2M1),
-                    rhs_scale=w4s[:, w : w + NT],
-                    start=start,
-                    stop=stop,
-                )
-            else:
-                nc.tensor.matmul_mx(
-                    out=acc[jc, nh][:],
-                    lhsT=h_c[jc][:].bitcast(E4M3),
-                    lhsT_scale=h_s[jc][:],
-                    rhs=uc[nh][:].bitcast(E4M3),
-                    rhs_scale=us[nh][:],
-                    start=start,
-                    stop=stop,
-                )
-
-        res = {}
-
-        def finish(jc, nh, engine):
-            res[jc, nh] = keep.tile([P, NT], F32, name=f"res{jc}{nh}")
-            copy_on(engine, res[jc, nh][:], acc[jc, nh][:])
-
-        def store(jc, nh):
-            nc.sync.dma_start(out[jc * P : (jc + 1) * P, nh * NT : (nh + 1) * NT], res[jc, nh][:])
-
-        xgg = {}
-        ug = {}
-        gather(1, 2, 0, g[1])
-        gather(0, 3, 0, g[0])
-        down_copy("S", 1, 0)
-        gather(1, 0, 0, g[1])
-        down_copy("S", 0, 0)
-        down_copy("V", 1, 1)
-        gather(0, 1, 0, g[0])
-        gather(1, 3, 0, g[1])
-        gather(1, 1, 0, g[1])
-        gather(0, 0, 0, g[0])
-        gather(0, 2, 0, g[0])
-        xgg[1, 0] = xg_copy("S", 1, 0)
-        down_copy("V", 0, 1)
-        xgg[0, 0] = xg_copy("S", 0, 0)
-        down_quant_all(1)
-        down_quant_all(0)
-        xg_quant(0, 0, xgg[0, 0])
-        xg_quant(1, 0, xgg[1, 0])
-        h_mm(0, 0 % 2)
-        h_copy("V", 0)
-        gather(1, 1, 1, g[1])
-        ug[0, 1] = up_copy("S", 0, 1)
-        gather(0, 0, 1, g[0])
-        gather(1, 3, 1, g[1])
-        gather(0, 1, 1, g[0])
-        gather(0, 2, 1, g[0])
-        gather(0, 3, 1, g[0])
-        xgg[0, 1] = xg_copy("S", 0, 1)
-        gather(1, 0, 1, g[1])
-        gather(1, 2, 1, g[1])
-        xgg[1, 1] = xg_copy("S", 1, 1)
-        xg_quant(0, 1, xgg[0, 1])
-        mm_pass(2, 0, 0, True, False)
-        xg_quant(1, 1, xgg[1, 1])
-        h_mm(2, 2 % 2)
-        up_quant(0, 1, ug[0, 1])
-        ug[0, 0] = up_copy("V", 0, 0)
-        mm_pass(2, 0, 1, False, False)
-        h_copy("S", 2)
-        up_quant(0, 0, ug[0, 0])
-        h_quant(2, hg[2])
-        mm_pass(2, 0, 2, False, True)
-        finish(2, 0, "V")
-        h_quant(0, hg[0])
-        mm_pass(0, 0, 2, True, False)
-        mm_pass(3, 1, 1, True, False)
-        h_mm(1, 1 % 2)
-        h_copy("S", 1)
-        mm_pass(2, 1, 1, True, False)
-        h_quant(1, hg[1])
-        mm_pass(1, 0, 0, True, False)
-        mm_pass(1, 0, 1, False, False)
-        mm_pass(1, 0, 2, False, True)
-        finish(1, 0, "S")
-        ug[1, 0] = up_copy("V", 1, 0)
-        ug[1, 1] = up_copy("V", 1, 1)
-        up_quant(1, 0, ug[1, 0])
-        up_quant(1, 1, ug[1, 1])
-        mm_pass(2, 1, 2, False, False)
-        mm_pass(2, 1, 0, False, True)
-        finish(2, 1, "S")
-        h_mm(3, 3 % 2)
-        mm_pass(0, 1, 2, True, False)
-        mm_pass(0, 1, 1, False, False)
-        mm_pass(0, 1, 0, False, True)
-        finish(0, 1, "V")
-        h_copy("S", 3)
-        h_quant(3, hg[3])
-        mm_pass(3, 0, 0, True, False)
-        store(2, 1)
-        mm_pass(3, 1, 2, False, False)
-        mm_pass(3, 1, 0, False, True)
-        finish(3, 1, "V")
-        mm_pass(0, 0, 1, False, False)
-        store(3, 1)
-        store(1, 0)
-        mm_pass(0, 0, 0, False, True)
-        mm_pass(3, 0, 1, False, False)
-        mm_pass(3, 0, 2, False, True)
-        mm_pass(1, 1, 1, True, False)
-        finish(0, 0, "S")
-        finish(3, 0, "S")
-        mm_pass(1, 1, 0, False, False)
-        mm_pass(1, 1, 2, False, True)
-        store(0, 1)
-        finish(1, 1, "S")
-        store(0, 0)
-        store(2, 0)
-        store(3, 0)
-        store(1, 1)
+        for part in range(2):
+            copy_up(vector, 1, part)
+        for part in range(2):
+            quantise_up(1, part)
+        for a in range(PASSES):
+            for jt in (2, 3):
+                multiply_w4(a, jt, 1)
+        for jt in (0, 1):
+            for a in range(PASSES):
+                multiply_w4(a, jt, 1)
+        for jt in (2, 3, 0, 1):
+            multiply_up(jt, 1)
+            finish(vector if jt in (0, 3) else scalar, jt, 1)

from contextlib import ExitStack

import concourse.mybir as mybir

K, R, M, T, S = 1024, 512, 1024, 1024, 512
FLOPS = 2 * (K * R * S + K * M * S + R * M * S)

F32 = mybir.dt.float32
BF16 = mybir.dt.bfloat16
I32 = mybir.dt.int32
U32 = mybir.dt.uint32
U16 = mybir.dt.uint16
U8 = mybir.dt.uint8
E4M3 = mybir.dt.float8_e4m3fn_x4
E2M1 = mybir.dt.float4_e2m1fn_x4
MULT = mybir.AluOpType.mult

P = 128
I4 = 4
PASSES = K // (P * I4)
LIST_HALF = S // 2
N_HALF = M // 2
COPY_COLUMNS = 256
R_HALF = R // 2
J_TILES = S // P


def tile_list_hlora_tm_none_kernel(tc, xT, w4_words, w4_scales, down, up, wgt, offs, out):
    nc = tc.nc
    with ExitStack() as ctx:
        lists = ctx.enter_context(tc.tile_pool(name="lists", bufs=1))
        keep = ctx.enter_context(tc.tile_pool(name="keep", bufs=1))
        psum = ctx.enter_context(tc.psum_pool(name="psum", bufs=1))

        offsets = lists.tile([P, S // 16], U16, name="offsets")
        nc.sync.dma_start(offsets[:], offs)

        w4_scale = keep.tile([P, PASSES * M], U8, name="w4_scale", align_bytes=64)
        nc.gpsimd.memset(w4_scale[:].bitcast(I32), 0)

        wgt_sb = keep.tile([P, S], F32, name="wgt_sb")
        planes = [[keep.tile([P, T], F32, name=f"plane{a}{i}") for i in range(I4)] for a in range(PASSES)]
        down_raw = [keep.tile([P, I4, R], F32, name=f"down_raw{a}") for a in range(PASSES)]
        up_raw = [keep.tile([P, I4, N_HALF], F32, name=f"up_raw{nh}") for nh in range(2)]
        w4_word = keep.tile([P, PASSES * 2 * M], U8, name="w4_word", align_bytes=64)

        x_rows = xT.rearrange("(a p i) t -> a i p t", a=PASSES, i=I4)
        down_rows = down.rearrange("(a p i) r -> a p i r", a=PASSES, i=I4)
        up_rows = up.rearrange("(p i) n -> p i n", i=I4)
        scale_rows = w4_scales.bitcast(I32).rearrange("a (q s) n -> s q a n", s=4)

        def load_plane(a, i):
            nc.sync.dma_start(planes[a][i][:], x_rows[a, i])

        def load_w4_scales():
            for s in range(4):
                rows = w4_scale[s:P:32, :].bitcast(I32)
                nc.sync.dma_start(rows.rearrange("q (a n) -> q a n", a=PASSES), scale_rows[s])

        load_plane(0, 0)
        nc.sync.dma_start(wgt_sb[:], wgt)
        for i in range(1, I4):
            load_plane(0, i)
        load_plane(1, 0)
        load_w4_scales()
        load_plane(1, 1)
        nc.sync.dma_start(down_raw[0][:], down_rows[0])
        load_plane(1, 2)
        load_plane(1, 3)
        nc.sync.dma_start(
            w4_word[:].bitcast(I32).rearrange("p (a n) -> p a n", a=PASSES),
            w4_words.bitcast(I32).rearrange("a p n -> p a n"),
        )
        nc.sync.dma_start(down_raw[1][:], down_rows[1])
        for nh in range(2):
            nc.sync.dma_start(up_raw[nh][:], up_rows[:, :, nh * N_HALF : (nh + 1) * N_HALF])

        xg_code, xg_scale, down_code, down_scale = [], [], [], []
        for a in range(PASSES):
            xg_code.append(keep.tile([P, S], U32, name=f"xg_code{a}", align_bytes=64))
            xg_scale.append(keep.tile([P, S], U8, name=f"xg_scale{a}", align_bytes=64))
        for a in range(PASSES):
            down_code.append(keep.tile([P, R], U32, name=f"down_code{a}", align_bytes=64))
            down_scale.append(keep.tile([P, R], U8, name=f"down_scale{a}", align_bytes=64))
        picked = [[keep.tile([P, I4, LIST_HALF], F32, name=f"picked{a}{half}") for half in range(2)] for a in range(PASSES)]
        down_bf = [keep.tile([P, I4, P, I4], BF16, name=f"down_bf{a}", align_bytes=64) for a in range(PASSES)]
        h_bf = [keep.tile([P, P, I4], BF16, name=f"h_bf{jt}", align_bytes=64) for jt in range(J_TILES)]
        h_code = [keep.tile([P, P], U32, name=f"h_code{jt}", align_bytes=64) for jt in range(J_TILES)]
        h_scale = [keep.tile([P, P], U8, name=f"h_scale{jt}", align_bytes=64) for jt in range(J_TILES)]
        up_code = [keep.tile([P, N_HALF], U32, name=f"up_code{nh}", align_bytes=64) for nh in range(2)]
        up_scale = [keep.tile([P, N_HALF], U8, name=f"up_scale{nh}", align_bytes=64) for nh in range(2)]
        xg_bf, up_bf, h_sum, out_sum = {}, {}, {}, {}

        def quantise(code, scale, values):
            nc.vector.quantize_mx(out=code.bitcast(E4M3), scales=scale, in_=values)

        def interleave(copy, dst, src):
            copy(dst.rearrange("p (c e) i -> p c i e", e=4), src.rearrange("p i (c e) -> p c i e", e=4))

        def gather(a, i):
            for half in range(2):
                nc.vector.tensor_tensor(
                    picked[a][half][:, i, :],
                    planes[a][i][:].indirect(offsets[:, half * LIST_HALF // 16 : (half + 1) * LIST_HALF // 16]),
                    wgt_sb[:, half * LIST_HALF : (half + 1) * LIST_HALF],
                    MULT,
                )

        def copy_xg(copy, a, half):
            xg_bf[a, half] = keep.tile([P, LIST_HALF, I4], BF16, name=f"xg_bf{a}{half}", align_bytes=64)
            interleave(copy, xg_bf[a, half][:], picked[a][half][:])

        def quantise_xg(a, half):
            cols = slice(half * LIST_HALF, (half + 1) * LIST_HALF)
            quantise(xg_code[a][:, cols], xg_scale[a][:, cols], xg_bf[a, half][:].rearrange("p c i -> p (c i)"))

        def copy_down(copy, a, half):
            m = slice(half * R_HALF // I4, (half + 1) * R_HALF // I4)
            copy(
                down_bf[a][:].rearrange("p t m i -> p m t i")[:, m, :, :],
                down_raw[a][:].rearrange("p i (m t) -> p m t i", t=I4)[:, m, :, :],
            )

        def quantise_down(a):
            quantise(down_code[a][:], down_scale[a][:], down_bf[a][:].rearrange("p t m i -> p (t m i)"))

        def multiply_h(jt):
            j = slice(jt * P, (jt + 1) * P)
            h_sum[jt] = psum.tile([P, I4, P], F32, name=f"bank{jt % 2}")
            for t in range(I4):
                cols = slice(t * P, (t + 1) * P)
                for a in range(PASSES):
                    nc.tensor.matmul_mx(
                        out=h_sum[jt][:, t, :],
                        lhsT=down_code[a][:, cols].bitcast(E4M3),
                        lhsT_scale=down_scale[a][:, cols],
                        rhs=xg_code[a][:, j].bitcast(E4M3),
                        rhs_scale=xg_scale[a][:, j],
                        start=(a == 0),
                        stop=(a == PASSES - 1),
                    )

        def copy_h(copy, jt):
            copy(h_bf[jt][:], h_sum[jt][:].rearrange("p t j -> p j t"))

        def quantise_h(jt):
            quantise(h_code[jt][:], h_scale[jt][:], h_bf[jt][:].rearrange("p j t -> p (j t)"))

        def copy_up(copy, nh, part):
            up_bf[nh, part] = keep.tile([P, COPY_COLUMNS, I4], BF16, name=f"up_bf{nh}{part}", align_bytes=64)
            interleave(copy, up_bf[nh, part][:], up_raw[nh][:, :, part * COPY_COLUMNS : (part + 1) * COPY_COLUMNS])

        def quantise_up(nh, part):
            cols = slice(part * COPY_COLUMNS, (part + 1) * COPY_COLUMNS)
            quantise(up_code[nh][:, cols], up_scale[nh][:, cols], up_bf[nh, part][:].rearrange("p c i -> p (c i)"))

        def multiply_w4(a, jt, nh):
            if a == 0:
                out_sum[jt, nh] = psum.tile([P, N_HALF], F32, name=f"bank{jt + J_TILES * (1 - nh)}")
            j = slice(jt * P, (jt + 1) * P)
            w = a * M + nh * N_HALF
            nc.tensor.matmul_mx(
                out=out_sum[jt, nh][:],
                lhsT=xg_code[a][:, j].bitcast(E4M3),
                lhsT_scale=xg_scale[a][:, j],
                rhs=w4_word[:, 2 * w : 2 * (w + N_HALF)].bitcast(E2M1),
                rhs_scale=w4_scale[:, w : w + N_HALF],
                start=(a == 0),
                stop=False,
            )

        def multiply_up(jt, nh):
            nc.tensor.matmul_mx(
                out=out_sum[jt, nh][:],
                lhsT=h_code[jt][:].bitcast(E4M3),
                lhsT_scale=h_scale[jt][:],
                rhs=up_code[nh][:].bitcast(E4M3),
                rhs_scale=up_scale[nh][:],
                start=False,
                stop=True,
            )

        def finish(copy, jt, nh):
            result = keep.tile([P, N_HALF], F32, name=f"result{jt}{nh}")
            copy(result[:], out_sum[jt, nh][:])
            nc.sync.dma_start(out[jt * P : (jt + 1) * P, nh * N_HALF : (nh + 1) * N_HALF], result[:])

        scalar, vector = nc.scalar.copy, nc.vector.tensor_copy

        for i in range(I4):
            gather(0, i)
        for half in range(2):
            copy_xg(scalar, 0, half)
        gather(1, 0)
        gather(1, 1)
        for half in range(2):
            quantise_xg(0, half)
        for half in range(2):
            copy_down(scalar, 0, half)
        for jt in range(J_TILES):
            multiply_w4(0, jt, 0)
        gather(1, 2)
        gather(1, 3)
        quantise_down(0)
        copy_xg(scalar, 1, 0)
        copy_xg(vector, 1, 1)
        copy_down(scalar, 1, 0)
        copy_down(vector, 1, 1)
        for half in range(2):
            quantise_xg(1, half)
        quantise_down(1)
        for jt in range(J_TILES):
            multiply_w4(1, jt, 0)

        for jt in range(J_TILES):
            multiply_h(jt)
            copy_h(scalar, jt)
            quantise_h(jt)

        for part in range(2):
            copy_up(vector, 0, part)
        for part in range(2):
            quantise_up(0, part)
        for jt in range(J_TILES):
            multiply_up(jt, 0)
            finish(scalar, jt, 0)

        for part in range(2):
            copy_up(vector, 1, part)
        for part in range(2):
            quantise_up(1, part)
        for a in range(PASSES):
            for jt in (2, 3):
                multiply_w4(a, jt, 1)
        for jt in (0, 1):
            for a in range(PASSES):
                multiply_w4(a, jt, 1)
        for jt in (2, 3, 0, 1):
            multiply_up(jt, 1)
            finish(vector if jt in (0, 3) else scalar, jt, 1)
